import numpy as np
import ml_dtypes


def mxq(x, axis, fmt="e4m3"):
    dtype, down = {"e4m3": (ml_dtypes.float8_e4m3fn, 7), "e5m2": (ml_dtypes.float8_e5m2, 14)}[fmt]
    v = np.moveaxis(np.asarray(x, np.float32).astype(ml_dtypes.bfloat16).astype(np.float64), axis, -1)
    blocks = v.reshape(v.shape[:-1] + (-1, 32))
    amax = np.abs(blocks).max(-1, keepdims=True)
    byte = np.maximum(np.where(amax > 0, np.frexp(amax)[1] - 1 + 127, 0) - down, 1)
    scale = np.exp2(byte - 127.0)
    codes = (blocks / scale).astype(np.float32).astype(dtype).astype(np.float64)
    return np.moveaxis((codes * scale).reshape(v.shape), -1, axis)


WIDE = False


def mx_kscale(k):
    if not WIDE:
        return np.ones(k)
    levels = np.array([10, -10, 5, -5, 0])
    if k % 512:
        return np.exp2(np.random.permutation(np.resize(levels, k // 32))).repeat(32)
    a = np.empty((k // 512, 16))
    for p in range(k // 512):
        a[p, :8] = np.random.permutation(np.resize(levels, 8))
        for g in range(8):
            far = levels[np.abs(levels - a[p, g]) >= 10]
            a[p, g + 8] = far[np.random.randint(len(far))]
    return np.exp2(a.ravel()).repeat(32)


def f64(x):
    return np.asarray(x).astype(np.float64)


def striped(idx):
    return np.tile(idx.reshape(-1, 16).T, (8, 1)).astype(np.uint16)


def unstriped(offs):
    return offs[:16].T.reshape(-1).astype(np.int64)


def striped8(idx):
    return np.concatenate([x.reshape(-1, 16).T for x in idx]).astype(np.uint16)


def runs(offs, k):
    lists = np.stack([offs[16 * r : 16 * r + 16].T.reshape(-1) for r in range(8)]).astype(np.int64)
    return lists[np.arange(k) % 512 // 64]


def pack_weight(w):
    k, n = w.shape
    w = f64(np.asarray(w, np.float32).astype(ml_dtypes.bfloat16)).reshape(k // 32, 32, n)
    amax = np.abs(w).max(1)
    byte = np.clip(np.where(amax > 0, np.frexp(amax)[1] - 1 + 127 - 7, 1), 1, 254)
    scaled = (w * np.exp2(127.0 - byte)[:, None, :]).reshape(k, n).astype(np.float32)
    words = np.ascontiguousarray(scaled.reshape(k // 512, 128, 4, n).transpose(0, 1, 3, 2)).astype(ml_dtypes.float8_e4m3fn).view(np.uint8)
    return words, np.ascontiguousarray(byte.astype(np.uint8).reshape(k // 512, 16, n))


def unpack_weight(words, scales):
    g, p, n, _ = words.shape
    vals = np.ascontiguousarray(words).view(ml_dtypes.float8_e4m3fn).astype(np.float64) * np.repeat(np.exp2(scales.astype(np.float64) - 127.0), 8, axis=1)[..., None]
    return vals.transpose(0, 1, 3, 2).reshape(g * 512, n)


def sigmoid(v):
    return 1.0 / (1.0 + np.exp(-np.maximum(v, -700.0)))


K, T, S, N, H, G, W = 512, 2048, 512, 512, 512, 2048, 384


def setup_inputs():
    n = np.random.standard_normal
    s = mx_kscale(K)[:, None]
    u = mx_kscale(S)
    packed_xT = pack_weight(n((K, T)) * s)
    packed_dT = pack_weight(n((K, G)) / s)
    return {
        "x_words": packed_xT[0],
        "x_scales": packed_xT[1],
        "w1": (n((K, H)) / np.sqrt(K) / s).astype(np.float32),
        "d_words": packed_dT[0],
        "d_scales": packed_dT[1],
        "gn": (np.random.uniform(0.5, 1.5, (H, 1)) * u[:, None]).astype(np.float32),
        "w2": (n((H, N)) / np.sqrt(H) / u[:, None]).astype(np.float32),
        "offs": striped(np.random.permutation(T)[:S]),
        "k1": striped8(np.random.randint(0, G, (8, H))),
        "two": striped(np.random.permutation(T)[:S]),
        "n1": striped8(np.stack([np.random.permutation(S) for _ in range(8)])),
        "n2": striped8(np.stack([np.random.permutation(S) for _ in range(8)])),
        "n3": striped(np.random.permutation(S)[:W]),
        "n4": striped(np.random.permutation(S)[:W]),
    }


def reference(x_words, x_scales, w1, d_words, d_scales, gn, w2, offs, k1, two, n1, n2, n3, n4):
    xq = unpack_weight(x_words, x_scales)[:, unstriped(offs)]
    y = mxq(f64(w1), 0, "e4m3").T @ xq
    d_k1 = unpack_weight(d_words, d_scales)[np.arange(K)[:, None], runs(k1, K)]
    x_two = unpack_weight(x_words, x_scales)[:, unstriped(two)]
    d = 0.0625 * (d_k1.T @ x_two)
    z = f64(gn) * (y + (sigmoid(d[np.arange(H)[:, None], runs(n2, H)] - d)) * (y[np.arange(H)[:, None], runs(n1, H)] - y))
    h = mxq(f64(w2), 0, "e4m3").T @ mxq(z, 0, "e4m3")
    old = h[:, unstriped(n3)]
    pa = h[:, unstriped(n4)]
    ra = old * sigmoid(pa)
    out = h.copy()
    out[:, unstriped(n3)] = ra
    return out

@@ -1,0 +1,242 @@
+from contextlib import ExitStack
+
+import concourse.mybir as mybir
+
+K, T, S, N, H, G, W = 512, 2048, 512, 512, 512, 2048, 384
+FLOPS = 3 * 2 * 512 * 512 * 512
+
+F32 = mybir.dt.float32
+BF16 = mybir.dt.bfloat16
+I32 = mybir.dt.int32
+U32 = mybir.dt.uint32
+U16 = mybir.dt.uint16
+U8 = mybir.dt.uint8
+FP8X4 = mybir.dt.float8_e4m3fn_x4
+ALU = mybir.AluOpType
+ACT = mybir.ActivationFunctionType
+
+P = 128
+PACK = 4
+STEP = 512
+
+
+def tile_picked_twkeypullbkgate_none_p_kernel(
+    tc, x_words, x_scales, w1, d_words, d_scales, gn, w2, offs, k1, two, n1, n2, n3, n4, out
+):
+    nc = tc.nc
+    with ExitStack() as ctx:
+        keep = ctx.enter_context(tc.tile_pool(name="keep", bufs=1))
+        psum = ctx.enter_context(tc.psum_pool(name="psum", bufs=1))
+
+        def load_list(name, src):
+            t = keep.tile(list(src.shape), U16, name=name)
+            nc.sync.dma_start(t[:], src)
+            return t
+
+        def load_words(name, src, cols):
+            t = keep.tile([P, cols], I32, name=name, align_bytes=64)
+            nc.sync.dma_start(t[:], src[0].rearrange("p c r -> p (c r)").bitcast(I32))
+            return t
+
+        def load_weight(name, src):
+            t = keep.tile([P, PACK, src.shape[1]], F32, name=name)
+            nc.sync.dma_start(t[:], src.rearrange("(p j) c -> p j c", j=PACK))
+            return t
+
+        def gather(name, dtype, window, lst):
+            t = keep.tile([P, S], dtype, name=name, align_bytes=64)
+            nc.vector.tensor_copy(t[:], window.indirect(lst[:]))
+            return t
+
+        def quantize(name, grouped):
+            cols = grouped.shape[1] // PACK
+            codes = keep.tile([P, cols], U32, name=name + "_codes", align_bytes=64)
+            scales = keep.tile([P, cols], U8, name=name + "_scales", align_bytes=64)
+            nc.vector.quantize_mx(out=codes[:].bitcast(FP8X4), scales=scales[:], in_=grouped)
+            return codes, scales
+
+        def product(bank, lhs, tile_no, rhs):
+            cols = slice(tile_no * P, (tile_no + 1) * P)
+            nc.tensor.matmul_mx(
+                out=bank[:],
+                lhsT=lhs[0][:, cols].bitcast(FP8X4),
+                lhsT_scale=lhs[1][:, cols],
+                rhs=rhs[0][:].bitcast(FP8X4),
+                rhs_scale=rhs[1][:],
+                start=True,
+                stop=True,
+            )
+
+        ds_win = keep.tile([P, G], U8, name="ds_win", align_bytes=64)
+        xs_win = keep.tile([P, T], U8, name="xs_win", align_bytes=64)
+        nc.vector.memset(ds_win[:].bitcast(I32), 0)
+        nc.gpsimd.memset(xs_win[:].bitcast(I32), 0)
+
+        k1_t = load_list("k1_t", k1)
+        offs_t = load_list("offs_t", offs)
+        two_t = load_list("two_t", two)
+        gn_t = keep.tile([P, PACK], F32, name="gn_t")
+        nc.sync.dma_start(gn_t[:], gn.rearrange("(p t) o -> p (t o)", t=PACK))
+        for r in range(2):
+            nc.sync.dma_start(ds_win[r:P:16, :].bitcast(I32), d_scales[0, r:16:2, :].bitcast(I32))
+        xw_win = load_words("xw_win", x_words, T)
+        for r in range(4):
+            nc.sync.dma_start(xs_win[r:P:32, :].bitcast(I32), x_scales[0, r:16:4, :].bitcast(I32))
+        w1_raw = load_weight("w1_raw", w1)
+        w2_raw = load_weight("w2_raw", w2)
+        dw_win = load_words("dw_win", d_words, G)
+        n1_t = load_list("n1_t", n1)
+        n2_t = load_list("n2_t", n2)
+        n3_t = load_list("n3_t", n3)
+        n4_t = load_list("n4_t", n4)
+
+        ds_g = gather("ds_g", U8, ds_win[:], k1_t)
+        ds_dealt = keep.tile([P, H], U8, name="ds_dealt", align_bytes=64)
+        nc.vector.tensor_copy(
+            ds_dealt[:].rearrange("p (t m) -> p m t", t=PACK), ds_g[:].rearrange("p (m t) -> p m t", t=PACK)
+        )
+        for r in range(2):
+            nc.sync.dma_start(ds_dealt[2 + r : P : 32, :].bitcast(I32), ds_dealt[16 + r : P : 32, :].bitcast(I32))
+
+        xw_offs = gather("xw_offs", U32, xw_win[:].bitcast(U32), offs_t)
+        xs_offs = gather("xs_offs", U8, xs_win[:], offs_t)
+        xw_two = gather("xw_two", U32, xw_win[:].bitcast(U32), two_t)
+        xs_two = gather("xs_two", U8, xs_win[:], two_t)
+
+        half_gn = keep.tile([P, PACK], F32, name="half_gn")
+        nc.scalar.activation(half_gn[:], gn_t[:], ACT.Copy, scale=0.5)
+
+        w1_bf = keep.tile([P, K * PACK], BF16, name="w1_bf", align_bytes=64)
+        nc.scalar.activation(
+            w1_bf[:].rearrange("p (t m j) -> p m j t", t=PACK, j=PACK),
+            w1_raw[:].rearrange("p j (m t) -> p m j t", t=PACK),
+            ACT.Copy,
+        )
+        w1_q = quantize("w1", w1_bf[:])
+
+        w2_bf = keep.tile([P, N * PACK], BF16, name="w2_bf", align_bytes=64)
+        nc.scalar.activation(
+            w2_bf[:].rearrange("p (c i j) -> p c j i", i=4, j=PACK),
+            w2_raw[:].rearrange("p j (c i) -> p c j i", i=4),
+            ACT.Copy,
+        )
+
+        dw_g = gather("dw_g", U32, dw_win[:].bitcast(U32), k1_t)
+        dw_dealt = keep.tile([P, H], U32, name="dw_dealt", align_bytes=64)
+        nc.vector.tensor_copy(
+            dw_dealt[:].rearrange("p (t c i) -> p c t i", t=PACK, i=4),
+            dw_g[:].rearrange("p (c i t) -> p c t i", t=PACK, i=4),
+        )
+
+        y_win = []
+        for t in range(PACK):
+            bank = psum.tile([P, S], F32, name="y_bank", tag="bank%d" % (PACK + t))
+            product(bank, w1_q, t, (xw_offs, xs_offs))
+            y_t = keep.tile([P, S], F32, name="y_win%d" % t)
+            nc.scalar.activation(y_t[:], bank[:], ACT.Copy, scale=half_gn[:, t : t + 1])
+            y_win.append(y_t)
+
+        d_banks = []
+        for t in range(PACK):
+            bank = psum.tile([P, S], F32, name="d_bank", tag="bank%d" % t)
+            product(bank, (dw_dealt, ds_dealt), t, (xw_two, xs_two))
+            d_banks.append(bank)
+        w2_q = quantize("w2", w2_bf[:])
+
+        d_win = [keep.tile([P, S], F32, name="d_win%d" % t) for t in range(PACK)]
+        h_win = [keep.tile([P, S], F32, name="h_win%d" % m) for m in range(N // P)]
+        th_win = [keep.tile([P, S], F32, name="th_win%d" % m) for m in range(N // P)]
+        spans = [(0, 256), (256, 512)]
+        steps = []
+        for part, (c0, c1) in enumerate(spans):
+            per = STEP // (c1 - c0)
+            steps.extend((part, t0, t0 + per) for t0 in range(0, PACK, per))
+        up = [keep.tile([P, PACK, c1 - c0], F32, name="up%d" % c0) for c0, c1 in spans]
+        down = [keep.tile([P, PACK, c1 - c0], F32, name="down%d" % c0) for c0, c1 in spans]
+        diff, th, h_banks = {}, {}, {}
+
+        def fetch_d(step):
+            part, t0, t1 = steps[step]
+            c0, c1 = spans[part]
+            diff[step] = keep.tile([P, t1 - t0, c1 - c0], F32, name="diff%d" % step, tag="diff", bufs=8)
+            for t in range(t0, t1):
+                if part == 0:
+                    if t in (2, 3):
+                        nc.vector.tensor_scalar(d_win[t][:], d_banks[t][:], 0.0625, None, ALU.mult)
+                    else:
+                        nc.scalar.activation(d_win[t][:], d_banks[t][:], ACT.Copy, scale=0.0625)
+                nc.scalar.activation(diff[step][:, t - t0, :], d_win[t][:].indirect(n2_t[:, c0 // 16 : c1 // 16]), ACT.Copy)
+                nc.vector.tensor_tensor(diff[step][:, t - t0, :], diff[step][:, t - t0, :], d_win[t][:, c0:c1], ALU.subtract)
+
+        def gate(step):
+            th[step] = keep.tile(list(diff[step].shape), F32, name="th%d" % step)
+            nc.scalar.activation(th[step][:], diff[step][:], ACT.Tanh, scale=0.5)
+
+        def mix(step):
+            part, t0, t1 = steps[step]
+            c0, c1 = spans[part]
+            lst = n1_t[:, c0 // 16 : c1 // 16]
+            if step in (2, 3):
+                y_g = keep.tile([P, t1 - t0, c1 - c0], F32, name="y_g%d" % step, tag="diff", bufs=8)
+            else:
+                y_g = keep.tile([P, t1 - t0, c1 - c0], F32, name="y_g%d" % step)
+            for t in range(t0, t1):
+                if step in (2, 3):
+                    nc.scalar.activation(y_g[:, t - t0, :], y_win[t][:].indirect(lst), ACT.Copy)
+                else:
+                    nc.vector.tensor_copy(y_g[:, t - t0, :], y_win[t][:].indirect(lst))
+            nc.vector.scalar_tensor_tensor(up[part][:, t0:t1, :], th[step][:], 1.0, y_g[:], ALU.add, ALU.mult)
+            for t in range(t0, t1):
+                nc.vector.scalar_tensor_tensor(
+                    down[part][:, t, :], th[step][:, t - t0, :], 1.0, y_win[t][:, c0:c1], ALU.subtract, ALU.mult
+                )
+
+        def project(part):
+            c0, c1 = spans[part]
+            z_bf = keep.tile([P, (c1 - c0) * PACK], BF16, name="z_bf%d" % part, align_bytes=64)
+            nc.vector.tensor_tensor(
+                z_bf[:].rearrange("p (c i t) -> p c t i", i=4, t=PACK),
+                up[part][:].rearrange("p t (c i) -> p c t i", i=4),
+                down[part][:].rearrange("p t (c i) -> p c t i", i=4),
+                ALU.subtract,
+            )
+            z_q = quantize("z%d" % part, z_bf[:])
+            for m in range(N // P):
+                bank = psum.tile([P, c1 - c0], F32, name="h_bank", tag="bank%d" % ((part * PACK + m) % 8))
+                product(bank, w2_q, m, z_q)
+                h_banks[part, m] = bank
+
+        def unload(part, m):
+            c0, c1 = spans[part]
+            if part < len(spans) - 1:
+                nc.scalar.copy(h_win[m][:, c0:c1], h_banks[part, m][:])
+                nc.scalar.activation(th_win[m][:, c0:c1], h_banks[part, m][:], ACT.Tanh, scale=0.5)
+            else:
+                nc.vector.tensor_copy(h_win[m][:, c0:c1], h_banks[part, m][:])
+                nc.scalar.activation(th_win[m][:, c0:c1], h_win[m][:, c0:c1], ACT.Tanh, scale=0.5)
+
+        fetch_d(0)
+        for step, (part, t0, t1) in enumerate(steps):
+            gate(step)
+            if step + 1 < len(steps):
+                fetch_d(step + 1)
+            mix(step)
+            if t1 == PACK:
+                project(part)
+
+        for part in range(len(spans) - 1):
+            for m in range(N // P):
+                unload(part, m)
+        olds = []
+        for m in range(N // P):
+            unload(len(spans) - 1, m)
+            old = keep.tile([P, W], F32, name="old%d" % m)
+            nc.scalar.activation(old[:], h_win[m][:].indirect(n3_t[:]), ACT.Copy, scale=0.5)
+            olds.append(old)
+        for m in range(N // P):
+            pa = keep.tile([P, W], F32, name="pa%d" % m)
+            nc.vector.tensor_copy(pa[:], th_win[m][:].indirect(n4_t[:]))
+            ra = keep.tile([P, W], F32, name="ra%d" % m)
+            nc.vector.scalar_tensor_tensor(ra[:], pa[:], 1.0, olds[m][:], ALU.add, ALU.mult)
+            nc.scalar.activation(h_win[m][:].indirect(n3_t[:]), ra[:], ACT.Copy)
+            nc.sync.dma_start(out[m * P : (m + 1) * P, :], h_win[m][:])

@@ -38,8 +38,8 @@ def tile_picked_twkeypullbkgate_none_p_kernel(
             nc.sync.dma_start(t[:], src[0].rearrange("p c r -> p (c r)").bitcast(I32))
             return t
 
-        def load_weight(name, src):
-            t = keep.tile([P, PACK, src.shape[1]], F32, name=name)
+        def load_weight(name, src, tag=None):
+            t = keep.tile([P, PACK, src.shape[1]], F32, name=name, tag=tag or name, align_bytes=64)
             nc.sync.dma_start(t[:], src.rearrange("(p j) c -> p j c", j=PACK))
             return t
 
@@ -73,8 +73,8 @@ def tile_picked_twkeypullbkgate_none_p_kernel(
         nc.gpsimd.memset(xs_win[:].bitcast(I32), 0)
 
         k1_t = load_list("k1_t", k1)
-        offs_t = load_list("offs_t", offs)
         two_t = load_list("two_t", two)
+        n2_t = load_list("n2_t", n2)
         gn_t = keep.tile([P, PACK], F32, name="gn_t")
         nc.sync.dma_start(gn_t[:], gn.rearrange("(p t) o -> p (t o)", t=PACK))
         for r in range(2):
@@ -82,13 +82,11 @@ def tile_picked_twkeypullbkgate_none_p_kernel(
         xw_win = load_words("xw_win", x_words, T)
         for r in range(4):
             nc.sync.dma_start(xs_win[r:P:32, :].bitcast(I32), x_scales[0, r:16:4, :].bitcast(I32))
-        w1_raw = load_weight("w1_raw", w1)
-        w2_raw = load_weight("w2_raw", w2)
         dw_win = load_words("dw_win", d_words, G)
+        w1_raw = [load_weight("w1_raw0", w1[:, : H // 2])]
+        offs_t = load_list("offs_t", offs)
+        w1_raw.append(load_weight("w1_raw1", w1[:, H // 2 :]))
         n1_t = load_list("n1_t", n1)
-        n2_t = load_list("n2_t", n2)
-        n3_t = load_list("n3_t", n3)
-        n4_t = load_list("n4_t", n4)
 
         ds_g = gather("ds_g", U8, ds_win[:], k1_t)
         ds_dealt = keep.tile([P, H], U8, name="ds_dealt", align_bytes=64)
@@ -97,50 +95,65 @@ def tile_picked_twkeypullbkgate_none_p_kernel(
         )
         for r in range(2):
             nc.sync.dma_start(ds_dealt[2 + r : P : 32, :].bitcast(I32), ds_dealt[16 + r : P : 32, :].bitcast(I32))
+        w2_raw = load_weight("w2_raw", w2, tag="ds_g")
+        n3_t = load_list("n3_t", n3)
+        n4_t = load_list("n4_t", n4)
 
-        xw_offs = gather("xw_offs", U32, xw_win[:].bitcast(U32), offs_t)
-        xs_offs = gather("xs_offs", U8, xs_win[:], offs_t)
         xw_two = gather("xw_two", U32, xw_win[:].bitcast(U32), two_t)
         xs_two = gather("xs_two", U8, xs_win[:], two_t)
-
-        half_gn = keep.tile([P, PACK], F32, name="half_gn")
-        nc.scalar.activation(half_gn[:], gn_t[:], ACT.Copy, scale=0.5)
-
-        w1_bf = keep.tile([P, K * PACK], BF16, name="w1_bf", align_bytes=64)
-        nc.scalar.activation(
-            w1_bf[:].rearrange("p (t m j) -> p m j t", t=PACK, j=PACK),
-            w1_raw[:].rearrange("p j (m t) -> p m j t", t=PACK),
-            ACT.Copy,
-        )
-        w1_q = quantize("w1", w1_bf[:])
-
-        w2_bf = keep.tile([P, N * PACK], BF16, name="w2_bf", align_bytes=64)
-        nc.scalar.activation(
-            w2_bf[:].rearrange("p (c i j) -> p c j i", i=4, j=PACK),
-            w2_raw[:].rearrange("p j (c i) -> p c j i", i=4),
-            ACT.Copy,
-        )
-
         dw_g = gather("dw_g", U32, dw_win[:].bitcast(U32), k1_t)
         dw_dealt = keep.tile([P, H], U32, name="dw_dealt", align_bytes=64)
         nc.vector.tensor_copy(
             dw_dealt[:].rearrange("p (t c i) -> p c t i", t=PACK, i=4),
             dw_g[:].rearrange("p (c i t) -> p c t i", t=PACK, i=4),
         )
+        xw_offs = gather("xw_offs", U32, xw_win[:].bitcast(U32), offs_t)
+        xs_offs = gather("xs_offs", U8, xs_win[:], offs_t)
 
-        y_win = []
-        for t in range(PACK):
-            bank = psum.tile([P, S], F32, name="y_bank", tag="bank%d" % (PACK + t))
-            product(bank, w1_q, t, (xw_offs, xs_offs))
-            y_t = keep.tile([P, S], F32, name="y_win%d" % t)
-            nc.scalar.activation(y_t[:], bank[:], ACT.Copy, scale=half_gn[:, t : t + 1])
-            y_win.append(y_t)
+        half_gn = keep.tile([P, PACK], F32, name="half_gn")
+        nc.scalar.activation(half_gn[:], gn_t[:], ACT.Copy, scale=0.5)
 
-        d_banks = []
+        def cast(engine, dst, src):
+            if engine == "g":
+                nc.gpsimd.tensor_scalar(dst, src, 1.0, 0.0, ALU.mult, ALU.add)
+            else:
+                nc.scalar.activation(dst, src, ACT.Copy)
+
+        w1_bf = keep.tile([P, K * PACK], BF16, name="w1_bf", align_bytes=64)
+        for half in range(2):
+            cast(
+                "sg"[half],
+                w1_bf[:].rearrange("p (t m j) -> p m j t", t=PACK, j=PACK)[:, half * 64 : (half + 1) * 64],
+                w1_raw[half][:].rearrange("p j (m t) -> p m j t", t=PACK),
+            )
+        w1_q = quantize("w1", w1_bf[:])
+
+        w2_bf = keep.tile([P, N * PACK], BF16, name="w2_bf", align_bytes=64)
+        for c0 in range(0, N, N // 4):
+            c1 = c0 + N // 4
+            cast(
+                "gggg"[c0 * 4 // N],
+                w2_bf[:, c0 * PACK : c1 * PACK].rearrange("p (c i j) -> p c j i", i=4, j=PACK),
+                w2_raw[:, :, c0:c1].rearrange("p j (c i) -> p c j i", i=4),
+            )
+
+        d_banks, y_banks = [], []
         for t in range(PACK):
-            bank = psum.tile([P, S], F32, name="d_bank", tag="bank%d" % t)
+            bank = psum.tile([P, S], F32, name="d_bank", tag="bank%d" % (PACK + t))
             product(bank, (dw_dealt, ds_dealt), t, (xw_two, xs_two))
             d_banks.append(bank)
+        for t in range(PACK):
+            bank = psum.tile([P, S], F32, name="y_bank", tag="bank%d" % t)
+            product(bank, w1_q, t, (xw_offs, xs_offs))
+            y_banks.append(bank)
+        y_win = [keep.tile([P, S], F32, name="y_win%d" % t) for t in range(PACK)]
+
+        def unload_y(t):
+            if t in (0, 1):
+                nc.vector.tensor_scalar(y_win[t][:], y_banks[t][:], half_gn[:, t : t + 1], None, ALU.mult)
+            else:
+                nc.scalar.activation(y_win[t][:], y_banks[t][:], ACT.Copy, scale=half_gn[:, t : t + 1])
+
         w2_q = quantize("w2", w2_bf[:])
 
         d_win = [keep.tile([P, S], F32, name="d_win%d" % t) for t in range(PACK)]
@@ -158,15 +171,17 @@ def tile_picked_twkeypullbkgate_none_p_kernel(
         def fetch_d(step):
             part, t0, t1 = steps[step]
             c0, c1 = spans[part]
-            diff[step] = keep.tile([P, t1 - t0, c1 - c0], F32, name="diff%d" % step, tag="diff", bufs=8)
+            diff[step] = keep.tile([P, t1 - t0, c1 - c0], F32, name="diff%d" % step, tag=("a", "b", "c", "d")[step])
             for t in range(t0, t1):
                 if part == 0:
-                    if t in (2, 3):
+                    if t in ():
                         nc.vector.tensor_scalar(d_win[t][:], d_banks[t][:], 0.0625, None, ALU.mult)
                     else:
                         nc.scalar.activation(d_win[t][:], d_banks[t][:], ACT.Copy, scale=0.0625)
                 nc.scalar.activation(diff[step][:, t - t0, :], d_win[t][:].indirect(n2_t[:, c0 // 16 : c1 // 16]), ACT.Copy)
-                nc.vector.tensor_tensor(diff[step][:, t - t0, :], diff[step][:, t - t0, :], d_win[t][:, c0:c1], ALU.subtract)
+                nc.vector.scalar_tensor_tensor(
+                    diff[step][:, t - t0, :], d_banks[t][:, c0:c1], -0.0625, diff[step][:, t - t0, :], ALU.mult, ALU.add
+                )
 
         def gate(step):
             th[step] = keep.tile(list(diff[step].shape), F32, name="th%d" % step)
@@ -176,12 +191,12 @@ def tile_picked_twkeypullbkgate_none_p_kernel(
             part, t0, t1 = steps[step]
             c0, c1 = spans[part]
             lst = n1_t[:, c0 // 16 : c1 // 16]
-            if step in (2, 3):
-                y_g = keep.tile([P, t1 - t0, c1 - c0], F32, name="y_g%d" % step, tag="diff", bufs=8)
-            else:
-                y_g = keep.tile([P, t1 - t0, c1 - c0], F32, name="y_g%d" % step)
+            if part == 0:
+                for t in range(t0, t1):
+                    unload_y(t)
+            y_g = keep.tile([P, t1 - t0, c1 - c0], F32, name="y_g%d" % step, tag=("y0", "y1", "y2", "y3")[step])
             for t in range(t0, t1):
-                if step in (2, 3):
+                if part * PACK + t in (3, 4, 5, 6, 7):
                     nc.scalar.activation(y_g[:, t - t0, :], y_win[t][:].indirect(lst), ACT.Copy)
                 else:
                     nc.vector.tensor_copy(y_g[:, t - t0, :], y_win[t][:].indirect(lst))

from contextlib import ExitStack

import concourse.mybir as mybir

K, T, S, N, H, G, W = 512, 2048, 512, 512, 512, 2048, 384
FLOPS = 3 * 2 * 512 * 512 * 512

F32 = mybir.dt.float32
BF16 = mybir.dt.bfloat16
I32 = mybir.dt.int32
U32 = mybir.dt.uint32
U16 = mybir.dt.uint16
U8 = mybir.dt.uint8
FP8X4 = mybir.dt.float8_e4m3fn_x4
ALU = mybir.AluOpType
ACT = mybir.ActivationFunctionType

P = 128
PACK = 4
STEP = 512


def tile_picked_twkeypullbkgate_none_p_kernel(
    tc, x_words, x_scales, w1, d_words, d_scales, gn, w2, offs, k1, two, n1, n2, n3, n4, out
):
    nc = tc.nc
    with ExitStack() as ctx:
        keep = ctx.enter_context(tc.tile_pool(name="keep", bufs=1))
        psum = ctx.enter_context(tc.psum_pool(name="psum", bufs=1))

        def load_list(name, src):
            t = keep.tile(list(src.shape), U16, name=name)
            nc.sync.dma_start(t[:], src)
            return t

        def load_words(name, src, cols):
            t = keep.tile([P, cols], I32, name=name, align_bytes=64)
            nc.sync.dma_start(t[:], src[0].rearrange("p c r -> p (c r)").bitcast(I32))
            return t

        def load_weight(name, src, tag=None):
            t = keep.tile([P, PACK, src.shape[1]], F32, name=name, tag=tag or name, align_bytes=64)
            nc.sync.dma_start(t[:], src.rearrange("(p j) c -> p j c", j=PACK))
            return t

        def gather(name, dtype, window, lst):
            t = keep.tile([P, S], dtype, name=name, align_bytes=64)
            nc.vector.tensor_copy(t[:], window.indirect(lst[:]))
            return t

        def quantize(name, grouped):
            cols = grouped.shape[1] // PACK
            codes = keep.tile([P, cols], U32, name=name + "_codes", align_bytes=64)
            scales = keep.tile([P, cols], U8, name=name + "_scales", align_bytes=64)
            nc.vector.quantize_mx(out=codes[:].bitcast(FP8X4), scales=scales[:], in_=grouped)
            return codes, scales

        def product(bank, lhs, tile_no, rhs):
            cols = slice(tile_no * P, (tile_no + 1) * P)
            nc.tensor.matmul_mx(
                out=bank[:],
                lhsT=lhs[0][:, cols].bitcast(FP8X4),
                lhsT_scale=lhs[1][:, cols],
                rhs=rhs[0][:].bitcast(FP8X4),
                rhs_scale=rhs[1][:],
                start=True,
                stop=True,
            )

        ds_win = keep.tile([P, G], U8, name="ds_win", align_bytes=64)
        xs_win = keep.tile([P, T], U8, name="xs_win", align_bytes=64)
        nc.vector.memset(ds_win[:].bitcast(I32), 0)
        nc.gpsimd.memset(xs_win[:].bitcast(I32), 0)

        k1_t = load_list("k1_t", k1)
        two_t = load_list("two_t", two)
        n2_t = load_list("n2_t", n2)
        gn_t = keep.tile([P, PACK], F32, name="gn_t")
        nc.sync.dma_start(gn_t[:], gn.rearrange("(p t) o -> p (t o)", t=PACK))
        for r in range(2):
            nc.sync.dma_start(ds_win[r:P:16, :].bitcast(I32), d_scales[0, r:16:2, :].bitcast(I32))
        xw_win = load_words("xw_win", x_words, T)
        for r in range(4):
            nc.sync.dma_start(xs_win[r:P:32, :].bitcast(I32), x_scales[0, r:16:4, :].bitcast(I32))
        dw_win = load_words("dw_win", d_words, G)
        w1_raw = [load_weight("w1_raw0", w1[:, : H // 2])]
        offs_t = load_list("offs_t", offs)
        w1_raw.append(load_weight("w1_raw1", w1[:, H // 2 :]))
        n1_t = load_list("n1_t", n1)

        ds_g = gather("ds_g", U8, ds_win[:], k1_t)
        ds_dealt = keep.tile([P, H], U8, name="ds_dealt", align_bytes=64)
        nc.vector.tensor_copy(
            ds_dealt[:].rearrange("p (t m) -> p m t", t=PACK), ds_g[:].rearrange("p (m t) -> p m t", t=PACK)
        )
        for r in range(2):
            nc.sync.dma_start(ds_dealt[2 + r : P : 32, :].bitcast(I32), ds_dealt[16 + r : P : 32, :].bitcast(I32))
        w2_raw = load_weight("w2_raw", w2, tag="ds_g")
        n3_t = load_list("n3_t", n3)
        n4_t = load_list("n4_t", n4)

        xw_two = gather("xw_two", U32, xw_win[:].bitcast(U32), two_t)
        xs_two = gather("xs_two", U8, xs_win[:], two_t)
        dw_g = gather("dw_g", U32, dw_win[:].bitcast(U32), k1_t)
        dw_dealt = keep.tile([P, H], U32, name="dw_dealt", align_bytes=64)
        nc.vector.tensor_copy(
            dw_dealt[:].rearrange("p (t c i) -> p c t i", t=PACK, i=4),
            dw_g[:].rearrange("p (c i t) -> p c t i", t=PACK, i=4),
        )
        xw_offs = gather("xw_offs", U32, xw_win[:].bitcast(U32), offs_t)
        xs_offs = gather("xs_offs", U8, xs_win[:], offs_t)

        half_gn = keep.tile([P, PACK], F32, name="half_gn")
        nc.scalar.activation(half_gn[:], gn_t[:], ACT.Copy, scale=0.5)

        def cast(engine, dst, src):
            if engine == "g":
                nc.gpsimd.tensor_scalar(dst, src, 1.0, 0.0, ALU.mult, ALU.add)
            else:
                nc.scalar.activation(dst, src, ACT.Copy)

        w1_bf = keep.tile([P, K * PACK], BF16, name="w1_bf", align_bytes=64)
        for half in range(2):
            cast(
                "sg"[half],
                w1_bf[:].rearrange("p (t m j) -> p m j t", t=PACK, j=PACK)[:, half * 64 : (half + 1) * 64],
                w1_raw[half][:].rearrange("p j (m t) -> p m j t", t=PACK),
            )
        w1_q = quantize("w1", w1_bf[:])

        w2_bf = keep.tile([P, N * PACK], BF16, name="w2_bf", align_bytes=64)
        for c0 in range(0, N, N // 4):
            c1 = c0 + N // 4
            cast(
                "gggg"[c0 * 4 // N],
                w2_bf[:, c0 * PACK : c1 * PACK].rearrange("p (c i j) -> p c j i", i=4, j=PACK),
                w2_raw[:, :, c0:c1].rearrange("p j (c i) -> p c j i", i=4),
            )

        d_banks, y_banks = [], []
        for t in range(PACK):
            bank = psum.tile([P, S], F32, name="d_bank", tag="bank%d" % (PACK + t))
            product(bank, (dw_dealt, ds_dealt), t, (xw_two, xs_two))
            d_banks.append(bank)
        for t in range(PACK):
            bank = psum.tile([P, S], F32, name="y_bank", tag="bank%d" % t)
            product(bank, w1_q, t, (xw_offs, xs_offs))
            y_banks.append(bank)
        y_win = [keep.tile([P, S], F32, name="y_win%d" % t) for t in range(PACK)]

        def unload_y(t):
            if t in (0, 1):
                nc.vector.tensor_scalar(y_win[t][:], y_banks[t][:], half_gn[:, t : t + 1], None, ALU.mult)
            else:
                nc.scalar.activation(y_win[t][:], y_banks[t][:], ACT.Copy, scale=half_gn[:, t : t + 1])

        w2_q = quantize("w2", w2_bf[:])

        d_win = [keep.tile([P, S], F32, name="d_win%d" % t) for t in range(PACK)]
        h_win = [keep.tile([P, S], F32, name="h_win%d" % m) for m in range(N // P)]
        th_win = [keep.tile([P, S], F32, name="th_win%d" % m) for m in range(N // P)]
        spans = [(0, 256), (256, 512)]
        steps = []
        for part, (c0, c1) in enumerate(spans):
            per = STEP // (c1 - c0)
            steps.extend((part, t0, t0 + per) for t0 in range(0, PACK, per))
        up = [keep.tile([P, PACK, c1 - c0], F32, name="up%d" % c0) for c0, c1 in spans]
        down = [keep.tile([P, PACK, c1 - c0], F32, name="down%d" % c0) for c0, c1 in spans]
        diff, th, h_banks = {}, {}, {}

        def fetch_d(step):
            part, t0, t1 = steps[step]
            c0, c1 = spans[part]
            diff[step] = keep.tile([P, t1 - t0, c1 - c0], F32, name="diff%d" % step, tag=("a", "b", "c", "d")[step])
            for t in range(t0, t1):
                if part == 0:
                    if t in ():
                        nc.vector.tensor_scalar(d_win[t][:], d_banks[t][:], 0.0625, None, ALU.mult)
                    else:
                        nc.scalar.activation(d_win[t][:], d_banks[t][:], ACT.Copy, scale=0.0625)
                nc.scalar.activation(diff[step][:, t - t0, :], d_win[t][:].indirect(n2_t[:, c0 // 16 : c1 // 16]), ACT.Copy)
                nc.vector.scalar_tensor_tensor(
                    diff[step][:, t - t0, :], d_banks[t][:, c0:c1], -0.0625, diff[step][:, t - t0, :], ALU.mult, ALU.add
                )

        def gate(step):
            th[step] = keep.tile(list(diff[step].shape), F32, name="th%d" % step)
            nc.scalar.activation(th[step][:], diff[step][:], ACT.Tanh, scale=0.5)

        def mix(step):
            part, t0, t1 = steps[step]
            c0, c1 = spans[part]
            lst = n1_t[:, c0 // 16 : c1 // 16]
            if part == 0:
                for t in range(t0, t1):
                    unload_y(t)
            y_g = keep.tile([P, t1 - t0, c1 - c0], F32, name="y_g%d" % step, tag=("y0", "y1", "y2", "y3")[step])
            for t in range(t0, t1):
                if part * PACK + t in (3, 4, 5, 6, 7):
                    nc.scalar.activation(y_g[:, t - t0, :], y_win[t][:].indirect(lst), ACT.Copy)
                else:
                    nc.vector.tensor_copy(y_g[:, t - t0, :], y_win[t][:].indirect(lst))
            nc.vector.scalar_tensor_tensor(up[part][:, t0:t1, :], th[step][:], 1.0, y_g[:], ALU.add, ALU.mult)
            for t in range(t0, t1):
                nc.vector.scalar_tensor_tensor(
                    down[part][:, t, :], th[step][:, t - t0, :], 1.0, y_win[t][:, c0:c1], ALU.subtract, ALU.mult
                )

        def project(part):
            c0, c1 = spans[part]
            z_bf = keep.tile([P, (c1 - c0) * PACK], BF16, name="z_bf%d" % part, align_bytes=64)
            nc.vector.tensor_tensor(
                z_bf[:].rearrange("p (c i t) -> p c t i", i=4, t=PACK),
                up[part][:].rearrange("p t (c i) -> p c t i", i=4),
                down[part][:].rearrange("p t (c i) -> p c t i", i=4),
                ALU.subtract,
            )
            z_q = quantize("z%d" % part, z_bf[:])
            for m in range(N // P):
                bank = psum.tile([P, c1 - c0], F32, name="h_bank", tag="bank%d" % ((part * PACK + m) % 8))
                product(bank, w2_q, m, z_q)
                h_banks[part, m] = bank

        def unload(part, m):
            c0, c1 = spans[part]
            if part < len(spans) - 1:
                nc.scalar.copy(h_win[m][:, c0:c1], h_banks[part, m][:])
                nc.scalar.activation(th_win[m][:, c0:c1], h_banks[part, m][:], ACT.Tanh, scale=0.5)
            else:
                nc.vector.tensor_copy(h_win[m][:, c0:c1], h_banks[part, m][:])
                nc.scalar.activation(th_win[m][:, c0:c1], h_win[m][:, c0:c1], ACT.Tanh, scale=0.5)

        fetch_d(0)
        for step, (part, t0, t1) in enumerate(steps):
            gate(step)
            if step + 1 < len(steps):
                fetch_d(step + 1)
            mix(step)
            if t1 == PACK:
                project(part)

        for part in range(len(spans) - 1):
            for m in range(N // P):
                unload(part, m)
        olds = []
        for m in range(N // P):
            unload(len(spans) - 1, m)
            old = keep.tile([P, W], F32, name="old%d" % m)
            nc.scalar.activation(old[:], h_win[m][:].indirect(n3_t[:]), ACT.Copy, scale=0.5)
            olds.append(old)
        for m in range(N // P):
            pa = keep.tile([P, W], F32, name="pa%d" % m)
            nc.vector.tensor_copy(pa[:], th_win[m][:].indirect(n4_t[:]))
            ra = keep.tile([P, W], F32, name="ra%d" % m)
            nc.vector.scalar_tensor_tensor(ra[:], pa[:], 1.0, olds[m][:], ALU.add, ALU.mult)
            nc.scalar.activation(h_win[m][:].indirect(n3_t[:]), ra[:], ACT.Copy)
            nc.sync.dma_start(out[m * P : (m + 1) * P, :], h_win[m][:])
